import numpy as np
import ml_dtypes


def mxq(x, axis, fmt="e4m3"):
    dtype, down = {"e4m3": (ml_dtypes.float8_e4m3fn, 7), "e5m2": (ml_dtypes.float8_e5m2, 14)}[fmt]
    v = np.moveaxis(np.asarray(x, np.float32).astype(ml_dtypes.bfloat16).astype(np.float64), axis, -1)
    blocks = v.reshape(v.shape[:-1] + (-1, 32))
    amax = np.abs(blocks).max(-1, keepdims=True)
    byte = np.maximum(np.where(amax > 0, np.frexp(amax)[1] - 1 + 127, 0) - down, 1)
    scale = np.exp2(byte - 127.0)
    codes = (blocks / scale).astype(np.float32).astype(dtype).astype(np.float64)
    return np.moveaxis((codes * scale).reshape(v.shape), -1, axis)


WIDE = False


def mx_kscale(k):
    if not WIDE:
        return np.ones(k)
    levels = np.array([10, -10, 5, -5, 0])
    if k % 512:
        return np.exp2(np.random.permutation(np.resize(levels, k // 32))).repeat(32)
    a = np.empty((k // 512, 16))
    for p in range(k // 512):
        a[p, :8] = np.random.permutation(np.resize(levels, 8))
        for g in range(8):
            far = levels[np.abs(levels - a[p, g]) >= 10]
            a[p, g + 8] = far[np.random.randint(len(far))]
    return np.exp2(a.ravel()).repeat(32)


def f64(x):
    return np.asarray(x).astype(np.float64)


def striped(idx):
    return np.tile(idx.reshape(-1, 16).T, (8, 1)).astype(np.uint16)


def unstriped(offs):
    return offs[:16].T.reshape(-1).astype(np.int64)


E2M1 = np.array([0.0, 0.5, 1.0, 1.5, 2.0, 3.0, 4.0, 6.0, -0.0, -0.5, -1.0, -1.5, -2.0, -3.0, -4.0, -6.0])


def pack_weight(w, fmt):
    k, n = w.shape
    w = f64(np.asarray(w, np.float32).astype(ml_dtypes.bfloat16)).reshape(k // 32, 32, n)
    amax = np.abs(w).max(1)
    if fmt == "e4m3":
        byte = np.frexp(amax)[1] - 1 + 127 - 7
    else:
        mant, ex = np.frexp(amax / 6.0)
        byte = np.where(mant > 0.5, ex, ex - 1) + 127
    byte = np.clip(np.where(amax > 0, byte, 1), 1, 254)
    scaled = (w * np.exp2(127.0 - byte)[:, None, :]).reshape(k, n).astype(np.float32)
    by_word = np.ascontiguousarray(scaled.reshape(k // 512, 128, 4, n).transpose(0, 1, 3, 2))
    if fmt == "e4m3":
        words = by_word.astype(ml_dtypes.float8_e4m3fn).view(np.uint8)
    else:
        c = by_word.astype(ml_dtypes.float4_e2m1fn).view(np.uint8) & 0xF
        words = (c[..., 0::2] | (c[..., 1::2] << 4)).reshape(k // 512, 128, 2 * n)
    return np.ascontiguousarray(words), np.ascontiguousarray(byte.astype(np.uint8).reshape(k // 512, 16, n))


def unpack_weight(words, scales, fmt):
    g, _, n = scales.shape
    words = np.ascontiguousarray(words).reshape(g, 128, n, -1)
    if fmt == "e4m3":
        vals = words.view(ml_dtypes.float8_e4m3fn).astype(np.float64)
    else:
        nib = np.empty((g, 128, n, 4), np.uint8)
        nib[..., 0::2] = words & 0xF
        nib[..., 1::2] = words >> 4
        vals = E2M1[nib]
    vals = vals * np.repeat(np.exp2(scales.astype(np.float64) - 127.0), 8, axis=1)[..., None]
    return vals.transpose(0, 1, 3, 2).reshape(g * 512, n)


def gelu(v):
    return 0.5 * v * (1.0 + np.tanh(np.sqrt(2.0 / np.pi) * (v + 0.044715 * v**3)))


K, K2, T, TB, S, P, H, N = 1024, 512, 4096, 2048, 1024, 512, 1024, 512

def setup_inputs():
    n = np.random.standard_normal
    s = mx_kscale(K)[:, None]
    s2 = mx_kscale(K2)[:, None]
    u = mx_kscale(H)[:, None]
    d = {}
    d["tab_words"], d["tab_scales"] = pack_weight(n((K, T)) * s, "e4m3")
    d["tab2_words"], d["tab2_scales"] = pack_weight(n((K2, TB)) * s2, "e4m3")
    d["offs"] = striped(np.random.permutation(T)[:S])
    d["offs2"] = striped(np.random.permutation(TB)[:P])
    d["pos1"] = striped(np.random.permutation(S)[:P])
    d["w1_words"], d["w1_scales"] = pack_weight(2.0 * n((K, H)) / K ** 0.5 / s, "e2m1")
    d["gain"] = (2.0 * np.exp(0.3 * n(H)) * u[:, 0]).astype(np.float32)
    d["w2"] = (n((K2, H)) / K2 ** 0.5 / s2 * u.T).astype(np.float32)
    d["micro"] = (n((H, P)) * u).astype(np.float32)
    d["wgs"] = np.exp(0.3 * n((128, P))).astype(np.float32)
    d["w3"] = (n((H, N)) / H ** 0.5 / u).astype(np.float32)
    d["lift"] = (0.6 * n(N)).astype(np.float32)
    return d

def reference(tab_words, tab_scales, tab2_words, tab2_scales, offs, offs2, pos1, w1_words, w1_scales, gain, w2, micro, wgs, w3, lift):
    v = unpack_weight(tab_words, tab_scales, "e4m3")[:, unstriped(offs)]
    v2 = unpack_weight(tab2_words, tab2_scales, "e4m3")[:, unstriped(offs2)]
    w1 = unpack_weight(w1_words, w1_scales, "e2m1")
    a = f64(gain)[:, None] / (1.0 + np.abs(w1.T @ v))
    b = (mxq(f64(w2), 0, "e4m3").T @ v2) + f64(micro)
    placed = np.zeros((H, S))
    placed[:, unstriped(pos1)] = np.tile(f64(wgs), (H // 128, 1)) * b
    z = a - placed
    y = mxq(f64(w3), 0, "e4m3").T @ mxq(z, 0, "e4m3")
    return y + f64(lift)[:, None] * np.abs(y)

@@ -1,0 +1,288 @@
+from contextlib import ExitStack
+
+import concourse.mybir as mybir
+
+K, K2, T, TB, S, PL, H, N = 1024, 512, 4096, 2048, 1024, 512, 1024, 512
+FLOPS = 2 * (K * H * S + K2 * H * PL + H * N * S)
+
+F32 = mybir.dt.float32
+BF16 = mybir.dt.bfloat16
+I32 = mybir.dt.int32
+U32 = mybir.dt.uint32
+U16 = mybir.dt.uint16
+U8 = mybir.dt.uint8
+E4M3 = mybir.dt.float8_e4m3fn_x4
+E2M1 = mybir.dt.float4_e2m1fn_x4
+ALU = mybir.AluOpType
+ACT = mybir.ActivationFunctionType
+
+P = 128
+PACK = 4
+PASS = P * PACK
+BANK = 512
+SLICES = H // P
+PAGES = 4
+
+
+def tile_list_saffron_adulteration_scores_kernel(
+    tc, tab_words, tab_scales, tab2_words, tab2_scales, offs, offs2, pos1,
+    w1_words, w1_scales, gain, w2, micro, wgs, w3, lift, out,
+):
+    nc = tc.nc
+    with ExitStack() as ctx:
+        lists = ctx.enter_context(tc.tile_pool(name="lists", bufs=1))
+        keep = ctx.enter_context(tc.tile_pool(name="keep", bufs=1))
+        two = ctx.enter_context(tc.tile_pool(name="two", bufs=2))
+        four = ctx.enter_context(tc.tile_pool(name="four", bufs=4))
+        ps_a = ctx.enter_context(tc.psum_pool(name="ps_a", bufs=4))
+        ps_b = ctx.enter_context(tc.psum_pool(name="ps_b", bufs=2))
+        ps_c = ctx.enter_context(tc.psum_pool(name="ps_c", bufs=2))
+
+        offs_sb = lists.tile([P, S // 16], U16, name="offs_sb")
+        offs2_sb = lists.tile([P, PL // 16], U16, name="offs2_sb")
+        pos_sb = lists.tile([P, PL // 16], U16, name="pos_sb")
+
+        def held(shape, dtype, name):
+            return keep.tile(shape, dtype, name=name, align_bytes=64)
+
+        tab2_s = held([P, TB], U8, "tab2_s")
+        tab_s = held([P, T], U8, "tab_s")
+        w1_s_raw = held([P, H], U8, "w1_s_raw")
+        tab2_w = held([P, TB], I32, "tab2_w")
+        w1_w_raw = held([P, 2, 2 * H], U8, "w1_w_raw")
+        gain_sb = held([P, 2, PACK], F32, "gain_sb")
+        lift_sb = held([P, N // P], F32, "lift_sb")
+        warm = held([P, 1], F32, "warm")
+        warm_out = held([P, 1], F32, "warm_out")
+        wgs_sb = [held([P, 2, PL], F32, f"wgs{u}") for u in range(2)]
+        pages = [held([P, S], F32, f"page{i}") for i in range(PAGES)]
+        tab_w = [two.tile([P, T], I32, name=f"tab_w{a}", tag="big", align_bytes=64) for a in range(2)]
+        micro_first = held([P, PL], F32, "micro_first")
+        after_tab0 = two.tile([P, SLICES - 1 + PACK, BANK], F32, name="after_tab0", tag="big", align_bytes=64)
+        after_tab1 = two.tile([P, 2 * PACK, BANK], F32, name="after_tab1", tag="big", align_bytes=64)
+        micro_sb = [micro_first[:]] + [after_tab0[:, i, :] for i in range(SLICES - 1)]
+        w2_first = held([P, PACK, PASS], F32, "w2_first")
+        w2_raw = [w2_first[:], after_tab1[:, 0:PACK, :]]
+        w3_raw = [after_tab1[:, PACK:2 * PACK, :], after_tab0[:, SLICES - 1:SLICES - 1 + PACK, :]]
+
+
+        def zero_upper(engine, tile):
+            words = tile[:].bitcast(I32)
+            engine.memset(words[32:64, :], 0)
+            engine.memset(words[64:128, :], 0)
+
+        micro_rows = micro.rearrange("(b p t) j -> b t p j", b=2, t=PACK)
+        wgs_rows = wgs.rearrange("(q u t) j -> u q t j", u=2, t=2)
+
+        def load_w2(b):
+            nc.sync.dma_start(w2_raw[b], w2[:, b * PASS:(b + 1) * PASS].rearrange("(p j) c -> p j c", j=PACK))
+
+        def load_wgs(u, q):
+            if True:
+                nc.sync.dma_start(wgs_sb[u][32 * q:32 * (q + 1)], wgs_rows[u])
+
+        def load_micro(i):
+            nc.sync.dma_start(micro_sb[i], micro_rows[i // PACK, i % PACK])
+
+        def load_tab(a):
+            nc.sync.dma_start(tab_w[a][:], tab_words[a].rearrange("p t i -> p (t i)").bitcast(I32))
+
+        nc.gpsimd.memset(warm[:], 1.0)
+        nc.scalar.activation(warm_out[:], warm[:], ACT.Abs_reciprocal_sqrt)
+        zero_upper(nc.vector, tab_s)
+        nc.gpsimd.memset(tab2_s[:].bitcast(I32), 0)
+        zero_upper(nc.gpsimd, w1_s_raw)
+        nc.sync.dma_start(offs2_sb[:], offs2)
+        nc.sync.dma_start(offs_sb[:], offs)
+        nc.sync.dma_start(tab_s[:].bitcast(I32)[0:32, :], tab_scales.bitcast(I32).rearrange("a q n -> q a n"))
+        nc.sync.dma_start(w1_s_raw[:].bitcast(I32)[0:32, :], w1_scales.bitcast(I32).rearrange("a q n -> q a n"))
+        nc.sync.dma_start(tab2_w[:], tab2_words[0].rearrange("p t i -> p (t i)").bitcast(I32))
+        load_w2(0)
+        load_micro(0)
+        load_wgs(0, 0)
+        for q in range(4):
+            nc.sync.dma_start(tab2_s[:].bitcast(I32)[32 * q:32 * q + 4, :], tab2_scales[0, 4 * q:4 * q + 4, :].bitcast(I32))
+        load_wgs(0, 2)
+        nc.sync.dma_start(w1_w_raw[:].bitcast(I32), w1_words.bitcast(I32).rearrange("a p n -> p a n"))
+        load_wgs(0, 1)
+        load_wgs(0, 3)
+        nc.sync.dma_start(pos_sb[:], pos1)
+        load_tab(0)
+        load_tab(1)
+        nc.sync.dma_start(gain_sb[:], gain.rearrange("(b p t) -> p b t", b=2, t=PACK))
+        for q in (0, 2, 1, 3):
+            load_wgs(1, q)
+        load_micro(1)
+        load_micro(2)
+        load_micro(3)
+        load_w2(1)
+        for i in range(PACK, SLICES):
+            load_micro(i)
+        for b in range(2):
+            nc.sync.dma_start(w3_raw[b], w3[b * PASS:(b + 1) * PASS, :].rearrange("(p j) n -> p j n", j=PACK))
+        with nc.allow_non_contiguous_dma("one value of lift for each partition"):
+            nc.sync.dma_start(lift_sb[:], lift.rearrange("(c p) -> p c", p=P))
+
+        v2_s = held([P, PL], U8, "v2_s")
+        planes = held([P, 2, S + H], U8, "planes")
+        nc.vector.memset(pages[0][:], 0.0)
+        nc.gpsimd.memset(planes[:].bitcast(I32), 0)
+
+        rows = held([P, S + H], U8, "rows")
+        v_s_rows = held([P, S], U8, "v_s_rows")
+        nc.vector.tensor_copy(v_s_rows[:], tab_s[:].indirect(offs_sb[:]))
+        nc.vector.tensor_copy(
+            rows[:, S:].rearrange("p (b t q) -> p b t q", b=2, t=PACK),
+            w1_s_raw[:].rearrange("p (b q t) -> p b t q", b=2, t=PACK),
+        )
+        nc.vector.tensor_copy(rows[:].bitcast(I32)[:, 0:S // 4], v_s_rows[:].bitcast(I32))
+        v2_w = held([P, PL], U32, "v2_w")
+        nc.vector.tensor_copy(v2_w[:], tab2_w[:].bitcast(U32).indirect(offs2_sb[:]))
+        nc.vector.tensor_copy(v2_s[:], tab2_s[:].indirect(offs2_sb[:]))
+        for q in range(4):
+            nc.gpsimd.dma_start(
+                planes[:].rearrange("p a c -> p (a c)").bitcast(I32)[32 * q:32 * q + 4, :],
+                rows[:].bitcast(I32)[8 * q:8 * (q + 1), :],
+            )
+        for i in range(1, PAGES):
+            nc.gpsimd.memset(pages[i][:], 0.0)
+        w1_w = held([P, 2, 2 * H], U8, "w1_w")
+        nc.vector.tensor_copy(
+            w1_w[:].rearrange("p a c -> p (a c)").bitcast(U16).rearrange("p (g t q) -> p g t q", g=4, t=PACK),
+            w1_w_raw[:].rearrange("p a c -> p (a c)").bitcast(U16).rearrange("p (g q t) -> p g t q", g=4, t=PACK),
+        )
+
+        w2_w = [held([P, PASS], U32, f"w2_w{b}") for b in range(2)]
+        w2_s = [held([P, PASS], U8, f"w2_s{b}") for b in range(2)]
+
+        def quantise_w2(b):
+            rounded = two.tile([P, PACK * PASS], BF16, name="rounded", tag="rounded", align_bytes=64)
+            dst = rounded[:].rearrange("p (t m j) -> p m t j", t=PACK, j=PACK)
+            src = w2_raw[b].rearrange("p j (m t) -> p m t j", t=PACK)
+            if b == 0:
+                nc.scalar.copy(dst[:, 0:P // 2], src[:, 0:P // 2])
+                nc.vector.tensor_copy(dst[:, P // 2:P], src[:, P // 2:P])
+            else:
+                nc.scalar.copy(dst, src)
+            nc.vector.quantize_mx(out=w2_w[b][:].bitcast(E4M3), scales=w2_s[b][:], in_=rounded[:])
+
+        w3_w = [held([P, N], U32, f"w3_w{b}") for b in range(2)]
+        w3_s = [held([P, N], U8, f"w3_s{b}") for b in range(2)]
+
+        def quantise_w3(b):
+            rounded = two.tile([P, PACK * N], BF16, name="rounded", tag="rounded", align_bytes=64)
+            nc.scalar.copy(
+                rounded[:].rearrange("p (c i j) -> p c j i", i=4, j=PACK),
+                w3_raw[b].rearrange("p j (c i) -> p c j i", i=4),
+            )
+            nc.vector.quantize_mx(out=w3_w[b][:].bitcast(E4M3), scales=w3_s[b][:], in_=rounded[:])
+
+        def findings(i):
+            b, t = divmod(i, PACK)
+            acc = ps_b.tile([P, BANK], F32, name="acc_b", tag="acc_b")
+            nc.tensor.matmul_mx(
+                out=acc[:], lhsT=w2_w[b][:, t * P:(t + 1) * P].bitcast(E4M3), lhsT_scale=w2_s[b][:, t * P:(t + 1) * P],
+                rhs=v2_w[:].bitcast(E4M3), rhs_scale=v2_s[:], start=True, stop=True,
+            )
+            summed = two.tile([P, PL], F32, name="summed", tag="summed")
+            nc.vector.tensor_tensor(summed[:], acc[:], micro_sb[i], ALU.add)
+            return summed
+
+        def place(i, summed):
+            nc.vector.tensor_tensor(pages[i % PAGES][:].indirect(pos_sb[:]), summed[:], wgs_sb[i % PACK // 2][:, i % 2, :], ALU.mult)
+
+        v_w = [held([P, S], U32, f"v_w{a}") for a in range(2)]
+
+        def gather_words(a, lo, hi):
+            nc.vector.tensor_copy(v_w[a][:, lo:hi], tab_w[a][:].bitcast(U32).indirect(offs_sb[:, lo // 16:hi // 16]))
+
+        mags = [held([P, S], F32, f"mag{i}") for i in range(2)]
+        roots = [held([P, S], F32, f"root{i}") for i in range(2)]
+
+        def response(i):
+            mag, root = mags[i % 2], roots[i % 2]
+            for h in range(2):
+                acc = ps_a.tile([P, BANK], F32, name="acc_a", tag="acc_a")
+                for a in range(2):
+                    nc.tensor.matmul_mx(
+                        out=acc[:],
+                        lhsT=w1_w[:, a, 2 * i * P:2 * (i + 1) * P].bitcast(E2M1),
+                        lhsT_scale=planes[:, a, S + i * P:S + (i + 1) * P],
+                        rhs=v_w[a][:, h * BANK:(h + 1) * BANK].bitcast(E4M3),
+                        rhs_scale=planes[:, a, h * BANK:(h + 1) * BANK],
+                        start=(a == 0), stop=(a == 1),
+                    )
+                nc.scalar.activation(mag[:, h * BANK:(h + 1) * BANK], acc[:], ACT.Abs)
+            nc.scalar.activation(root[:], mag[:], ACT.Abs_reciprocal_sqrt, bias=1.0)
+            recip = four.tile([P, S], F32, name="recip", tag="recip")
+            nc.scalar.activation(recip[:], root[:], ACT.Square)
+            return recip
+
+        z_rows = [held([P, PACK, S], BF16, f"z_rows{b}") for b in range(2)]
+
+        def subtract(i, recip):
+            b, t = divmod(i, PACK)
+            pieces = 2 if i == SLICES - 1 else 1
+            for u in range(pieces):
+                cols = slice(u * S // pieces, (u + 1) * S // pieces)
+                nc.vector.scalar_tensor_tensor(
+                    z_rows[b][:, t, cols], recip[:, cols], gain_sb[:, b, t:t + 1], pages[i % PAGES][:, cols],
+                    ALU.mult, ALU.subtract,
+                )
+
+        quantise_w2(0)
+        sums = {0: findings(0)}
+        place(0, sums[0])
+        gather_words(0, 0, S)
+        gather_words(1, 0, BANK)
+        gather_words(1, BANK, S)
+        for i in range(1, PAGES):
+            sums[i] = findings(i)
+            place(i, sums[i])
+        quantise_w2(1)
+        for i in range(SLICES):
+            recip = response(i)
+            if i + PAGES < SLICES:
+                sums[i + PAGES] = findings(i + PAGES)
+            subtract(i, recip)
+            if i + PAGES < SLICES:
+                place(i + PAGES, sums[i + PAGES])
+            if i in (2, 4):
+                quantise_w3(i // 2 - 1)
+
+        z_w = [held([P, S], U32, f"z_w{b}") for b in range(2)]
+        z_s = [held([P, S], U8, f"z_s{b}") for b in range(2)]
+        woven = {}
+        for b, h in ((0, 1), (0, 0), (1, 0), (1, 1)):
+            if True:
+                tile = (roots, mags)[h][1 - b]
+                woven[b, h] = tile[:].bitcast(BF16)
+                dst = woven[b, h].rearrange("p (c i t) -> p c t i", i=4, t=PACK)
+                src = z_rows[b][:, :, h * BANK:(h + 1) * BANK].rearrange("p t (c i) -> p c t i", i=4)
+                if (b, h) != (1, 1):
+                    nc.scalar.copy(dst, src)
+                else:
+                    nc.vector.tensor_copy(dst, src)
+        for b in range(2):
+            for h in (1, 0):
+                cols = slice(h * BANK, (h + 1) * BANK)
+                nc.vector.quantize_mx(out=z_w[b][:, cols].bitcast(E4M3), scales=z_s[b][:, cols], in_=woven[b, h])
+
+        result = two.tile([P, 2 * (N // P), BANK], F32, name="result", tag="big", align_bytes=64)
+        absolute = two.tile([P, 2 * (N // P), BANK], F32, name="absolute", tag="big", align_bytes=64)
+        banks = [(ps_c, "acc_c")] * 2 + [(ps_b, "acc_b")] * 2 + [(ps_a, "acc_a")] * 4
+        units = [(h, c) for h in (1, 0) for c in range(N // P)]
+        accs = [pool.tile([P, BANK], F32, name=tag, tag=tag) for pool, tag in banks]
+        for b in range(2):
+            for u, (h, c) in enumerate(units):
+                cols = slice(h * BANK, (h + 1) * BANK)
+                nc.tensor.matmul_mx(
+                    out=accs[u][:], lhsT=w3_w[b][:, c * P:(c + 1) * P].bitcast(E4M3), lhsT_scale=w3_s[b][:, c * P:(c + 1) * P],
+                    rhs=z_w[b][:, cols].bitcast(E4M3), rhs_scale=z_s[b][:, cols], start=(b == 0), stop=(b == 1),
+                )
+        for u, (h, c) in enumerate(units):
+            nc.scalar.activation(absolute[:, u, :], accs[u][:], ACT.Abs)
+            nc.vector.scalar_tensor_tensor(
+                result[:, u, :], absolute[:, u, :], lift_sb[:, c:c + 1], accs[u][:], ALU.mult, ALU.add,
+            )
+            nc.sync.dma_start(out[c * P:(c + 1) * P, h * BANK:(h + 1) * BANK], result[:, u, :])

@@ -1,6 +1,7 @@
 from contextlib import ExitStack
 
 import concourse.mybir as mybir
+from concourse.masks import make_identity
 
 K, K2, T, TB, S, PL, H, N = 1024, 512, 4096, 2048, 1024, 512, 1024, 512
 FLOPS = 2 * (K * H * S + K2 * H * PL + H * N * S)
@@ -33,6 +34,7 @@ def tile_list_saffron_adulteration_scores_kernel(
         lists = ctx.enter_context(tc.tile_pool(name="lists", bufs=1))
         keep = ctx.enter_context(tc.tile_pool(name="keep", bufs=1))
         two = ctx.enter_context(tc.tile_pool(name="two", bufs=2))
+        shared = ctx.enter_context(tc.tile_pool(name="shared", bufs=1))
         four = ctx.enter_context(tc.tile_pool(name="four", bufs=4))
         ps_a = ctx.enter_context(tc.psum_pool(name="ps_a", bufs=4))
         ps_b = ctx.enter_context(tc.psum_pool(name="ps_b", bufs=2))
@@ -50,21 +52,25 @@ def tile_list_saffron_adulteration_scores_kernel(
         w1_s_raw = held([P, H], U8, "w1_s_raw")
         tab2_w = held([P, TB], I32, "tab2_w")
         w1_w_raw = held([P, 2, 2 * H], U8, "w1_w_raw")
-        gain_sb = held([P, 2, PACK], F32, "gain_sb")
-        lift_sb = held([P, N // P], F32, "lift_sb")
         warm = held([P, 1], F32, "warm")
         warm_out = held([P, 1], F32, "warm_out")
-        wgs_sb = [held([P, 2, PL], F32, f"wgs{u}") for u in range(2)]
         pages = [held([P, S], F32, f"page{i}") for i in range(PAGES)]
-        tab_w = [two.tile([P, T], I32, name=f"tab_w{a}", tag="big", align_bytes=64) for a in range(2)]
-        micro_first = held([P, PL], F32, "micro_first")
-        after_tab0 = two.tile([P, SLICES - 1 + PACK, BANK], F32, name="after_tab0", tag="big", align_bytes=64)
-        after_tab1 = two.tile([P, 2 * PACK, BANK], F32, name="after_tab1", tag="big", align_bytes=64)
-        micro_sb = [micro_first[:]] + [after_tab0[:, i, :] for i in range(SLICES - 1)]
-        w2_first = held([P, PACK, PASS], F32, "w2_first")
-        w2_raw = [w2_first[:], after_tab1[:, 0:PACK, :]]
-        w3_raw = [after_tab1[:, PACK:2 * PACK, :], after_tab0[:, SLICES - 1:SLICES - 1 + PACK, :]]
 
+        def placed_at(offset, shape, dtype, name):
+            return shared.tile(shape, dtype, name=name, offset=offset, align_bytes=64)
+
+        row = 4 * BANK
+        tab_w = [placed_at(a * 8 * row, [P, T], I32, f"tab_w{a}") for a in range(2)]
+        micro_sb = [keep.tile([P, PL], F32, name=f"micro{i}", tag="micro_early")[:] for i in range(2)]
+        micro_sb = micro_sb + [placed_at(i * row, [P, PL], F32, f"micro{i}")[:] for i in range(2, PACK)]
+        wgs_sb = [held([P, PL], F32, f"wgs{t}") for t in range(PACK)]
+        gain_sb = placed_at(5 * row, [P, 2, PACK], F32, "gain_sb")
+        lift_sb = placed_at(5 * row + 64, [P, N // P], F32, "lift_sb")
+        w2_first = held([P, PACK, PASS], F32, "w2_first")
+        w2_raw = [w2_first[:], placed_at(6 * row, [P, PACK, PASS], F32, "w2_second")[:]]
+        micro_sb = micro_sb + [placed_at((6 + i) * row, [P, PL], F32, f"micro{i}")[:] for i in range(PACK, SLICES)]
+        w3_both = placed_at(14 * row, [P, 2, PACK, N], F32, "w3_both")
+        w3_raw = [w3_both[:, b] for b in range(2)]
 
         def zero_upper(engine, tile):
             words = tile[:].bitcast(I32)
@@ -72,14 +78,9 @@ def tile_list_saffron_adulteration_scores_kernel(
             engine.memset(words[64:128, :], 0)
 
         micro_rows = micro.rearrange("(b p t) j -> b t p j", b=2, t=PACK)
-        wgs_rows = wgs.rearrange("(q u t) j -> u q t j", u=2, t=2)
 
         def load_w2(b):
             nc.sync.dma_start(w2_raw[b], w2[:, b * PASS:(b + 1) * PASS].rearrange("(p j) c -> p j c", j=PACK))
-
-        def load_wgs(u, q):
-            if True:
-                nc.sync.dma_start(wgs_sb[u][32 * q:32 * (q + 1)], wgs_rows[u])
 
         def load_micro(i):
             nc.sync.dma_start(micro_sb[i], micro_rows[i // PACK, i % PACK])
@@ -88,31 +89,29 @@ def tile_list_saffron_adulteration_scores_kernel(
             nc.sync.dma_start(tab_w[a][:], tab_words[a].rearrange("p t i -> p (t i)").bitcast(I32))
 
         nc.gpsimd.memset(warm[:], 1.0)
-        nc.scalar.activation(warm_out[:], warm[:], ACT.Abs_reciprocal_sqrt)
-        zero_upper(nc.vector, tab_s)
         nc.gpsimd.memset(tab2_s[:].bitcast(I32), 0)
+        zero_upper(nc.vector, tab_s)
+        identity = held([P, P], F32, "identity")
+        make_identity(nc, identity[:])
         zero_upper(nc.gpsimd, w1_s_raw)
+        nc.scalar.activation(warm_out[:], warm[:], ACT.Abs_reciprocal_sqrt)
+        for q in range(4):
+            nc.scalar.dma_start(tab2_s[:].bitcast(I32)[32 * q:32 * q + 4, :], tab2_scales[0, 4 * q:4 * q + 4, :].bitcast(I32))
         nc.sync.dma_start(offs2_sb[:], offs2)
         nc.sync.dma_start(offs_sb[:], offs)
         nc.sync.dma_start(tab_s[:].bitcast(I32)[0:32, :], tab_scales.bitcast(I32).rearrange("a q n -> q a n"))
         nc.sync.dma_start(w1_s_raw[:].bitcast(I32)[0:32, :], w1_scales.bitcast(I32).rearrange("a q n -> q a n"))
-        nc.sync.dma_start(tab2_w[:], tab2_words[0].rearrange("p t i -> p (t i)").bitcast(I32))
-        load_w2(0)
-        load_micro(0)
-        load_wgs(0, 0)
-        for q in range(4):
-            nc.sync.dma_start(tab2_s[:].bitcast(I32)[32 * q:32 * q + 4, :], tab2_scales[0, 4 * q:4 * q + 4, :].bitcast(I32))
-        load_wgs(0, 2)
-        nc.sync.dma_start(w1_w_raw[:].bitcast(I32), w1_words.bitcast(I32).rearrange("a p n -> p a n"))
-        load_wgs(0, 1)
-        load_wgs(0, 3)
         nc.sync.dma_start(pos_sb[:], pos1)
+        wgs_raw = held([P, PL], F32, "wgs_raw")
+        nc.sync.dma_start(wgs_raw[:], wgs)
+        load_w2(0)
+        nc.sync.dma_start(tab2_w[:], tab2_words[0].rearrange("p t i -> p (t i)").bitcast(I32))
+        load_micro(0)
         load_tab(0)
+        nc.sync.dma_start(w1_w_raw[:].bitcast(I32), w1_words.bitcast(I32).rearrange("a p n -> p a n"))
         load_tab(1)
-        nc.sync.dma_start(gain_sb[:], gain.rearrange("(b p t) -> p b t", b=2, t=PACK))
-        for q in (0, 2, 1, 3):
-            load_wgs(1, q)
         load_micro(1)
+        nc.sync.dma_start(gain_sb[:], gain.rearrange("(b p t) -> p b t", b=2, t=PACK))
         load_micro(2)
         load_micro(3)
         load_w2(1)
@@ -125,22 +124,22 @@ def tile_list_saffron_adulteration_scores_kernel(
 
         v2_s = held([P, PL], U8, "v2_s")
         planes = held([P, 2, S + H], U8, "planes")
-        nc.vector.memset(pages[0][:], 0.0)
+        nc.gpsimd.memset(pages[0][:], 0.0)
         nc.gpsimd.memset(planes[:].bitcast(I32), 0)
 
         rows = held([P, S + H], U8, "rows")
         v_s_rows = held([P, S], U8, "v_s_rows")
         nc.vector.tensor_copy(v_s_rows[:], tab_s[:].indirect(offs_sb[:]))
+        v2_w = held([P, PL], U32, "v2_w")
+        nc.vector.tensor_copy(v2_s[:], tab2_s[:].indirect(offs2_sb[:]))
+        nc.vector.tensor_copy(v2_w[:], tab2_w[:].bitcast(U32).indirect(offs2_sb[:]))
         nc.vector.tensor_copy(
             rows[:, S:].rearrange("p (b t q) -> p b t q", b=2, t=PACK),
             w1_s_raw[:].rearrange("p (b q t) -> p b t q", b=2, t=PACK),
         )
         nc.vector.tensor_copy(rows[:].bitcast(I32)[:, 0:S // 4], v_s_rows[:].bitcast(I32))
-        v2_w = held([P, PL], U32, "v2_w")
-        nc.vector.tensor_copy(v2_w[:], tab2_w[:].bitcast(U32).indirect(offs2_sb[:]))
-        nc.vector.tensor_copy(v2_s[:], tab2_s[:].indirect(offs2_sb[:]))
         for q in range(4):
-            nc.gpsimd.dma_start(
+            nc.scalar.dma_start(
                 planes[:].rearrange("p a c -> p (a c)").bitcast(I32)[32 * q:32 * q + 4, :],
                 rows[:].bitcast(I32)[8 * q:8 * (q + 1), :],
             )
@@ -159,11 +158,7 @@ def tile_list_saffron_adulteration_scores_kernel(
             rounded = two.tile([P, PACK * PASS], BF16, name="rounded", tag="rounded", align_bytes=64)
             dst = rounded[:].rearrange("p (t m j) -> p m t j", t=PACK, j=PACK)
             src = w2_raw[b].rearrange("p j (m t) -> p m t j", t=PACK)
-            if b == 0:
-                nc.scalar.copy(dst[:, 0:P // 2], src[:, 0:P // 2])
-                nc.vector.tensor_copy(dst[:, P // 2:P], src[:, P // 2:P])
-            else:
-                nc.scalar.copy(dst, src)
+            nc.scalar.copy(dst, src)
             nc.vector.quantize_mx(out=w2_w[b][:].bitcast(E4M3), scales=w2_s[b][:], in_=rounded[:])
 
         w3_w = [held([P, N], U32, f"w3_w{b}") for b in range(2)]
@@ -189,7 +184,7 @@ def tile_list_saffron_adulteration_scores_kernel(
             return summed
 
         def place(i, summed):
-            nc.vector.tensor_tensor(pages[i % PAGES][:].indirect(pos_sb[:]), summed[:], wgs_sb[i % PACK // 2][:, i % 2, :], ALU.mult)
+            nc.vector.tensor_tensor(pages[i % PAGES][:].indirect(pos_sb[:]), summed[:], wgs_sb[i % PACK][:], ALU.mult)
 
         v_w = [held([P, S], U32, f"v_w{a}") for a in range(2)]
 
@@ -230,7 +225,47 @@ def tile_list_saffron_adulteration_scores_kernel(
                     ALU.mult, ALU.subtract,
                 )
 
+        z_w = [held([P, S], U32, f"z_w{b}") for b in range(2)]
+        z_s = [held([P, S], U8, f"z_s{b}") for b in range(2)]
+
+        def weave(b, h, on_scalar):
+            woven = (roots, mags)[h][b][:].bitcast(BF16)
+            dst = woven.rearrange("p (c i t) -> p c t i", i=4, t=PACK)
+            src = z_rows[b][:, :, h * BANK:(h + 1) * BANK].rearrange("p t (c i) -> p c t i", i=4)
+            if on_scalar:
+                nc.scalar.copy(dst, src)
+            else:
+                nc.vector.tensor_copy(dst, src)
+
+        def quantise_z(b, h):
+            woven = (roots, mags)[h][b][:].bitcast(BF16)
+            cols = slice(h * BANK, (h + 1) * BANK)
+            nc.vector.quantize_mx(out=z_w[b][:, cols].bitcast(E4M3), scales=z_s[b][:, cols], in_=woven)
+
+        chunks = PL // P
+        turned = ps_c.tile([P, chunks, P], F32, name="acc_c", tag="acc_c")
+        for c in range(chunks):
+            nc.tensor.transpose(turned[:, c, :], wgs_raw[:, c * P:(c + 1) * P], identity[:])
+        dealt = held([P, PACK, chunks, P], F32, "dealt")
+
+        def deal_wgs(t):
+            nc.scalar.copy(
+                dealt[:, t].rearrange("p c (r q) -> p c r q", r=4),
+                turned[:].rearrange("p c (q t) -> p t c q", t=PACK)[:, t].unsqueeze(2).to_broadcast([P, chunks, 4, 32]),
+            )
+
+        def turn_back_wgs(t):
+            back = ps_a.tile([P, chunks, P], F32, name="acc_a", tag="acc_a")
+            for c in range(chunks):
+                nc.tensor.transpose(back[:, c, :], dealt[:, t, c, :], identity[:])
+            nc.scalar.copy(wgs_sb[t][:], back[:].rearrange("p c j -> p (c j)"))
+
+        deal_wgs(0)
         quantise_w2(0)
+        turn_back_wgs(0)
+        for t in range(1, PACK):
+            deal_wgs(t)
+            turn_back_wgs(t)
         sums = {0: findings(0)}
         place(0, sums[0])
         gather_words(0, 0, S)
@@ -241,6 +276,10 @@ def tile_list_saffron_adulteration_scores_kernel(
             place(i, sums[i])
         quantise_w2(1)
         for i in range(SLICES):
+            if i == SLICES - 1:
+                for h in (1, 0):
+                    weave(0, h, True)
+                    quantise_z(0, h)
             recip = response(i)
             if i + PAGES < SLICES:
                 sums[i + PAGES] = findings(i + PAGES)
@@ -249,27 +288,13 @@ def tile_list_saffron_adulteration_scores_kernel(
                 place(i + PAGES, sums[i + PAGES])
             if i in (2, 4):
                 quantise_w3(i // 2 - 1)
+        weave(1, 0, True)
+        weave(1, 1, False)
+        quantise_z(1, 1)
+        quantise_z(1, 0)
 
-        z_w = [held([P, S], U32, f"z_w{b}") for b in range(2)]
-        z_s = [held([P, S], U8, f"z_s{b}") for b in range(2)]
-        woven = {}
-        for b, h in ((0, 1), (0, 0), (1, 0), (1, 1)):
-            if True:
-                tile = (roots, mags)[h][1 - b]
-                woven[b, h] = tile[:].bitcast(BF16)
-                dst = woven[b, h].rearrange("p (c i t) -> p c t i", i=4, t=PACK)
-                src = z_rows[b][:, :, h * BANK:(h + 1) * BANK].rearrange("p t (c i) -> p c t i", i=4)
-                if (b, h) != (1, 1):
-                    nc.scalar.copy(dst, src)
-                else:
-                    nc.vector.tensor_copy(dst, src)
-        for b in range(2):
-            for h in (1, 0):
-                cols = slice(h * BANK, (h + 1) * BANK)
-                nc.vector.quantize_mx(out=z_w[b][:, cols].bitcast(E4M3), scales=z_s[b][:, cols], in_=woven[b, h])
-
-        result = two.tile([P, 2 * (N // P), BANK], F32, name="result", tag="big", align_bytes=64)
-        absolute = two.tile([P, 2 * (N // P), BANK], F32, name="absolute", tag="big", align_bytes=64)
+        result = placed_at(6 * row, [P, 2 * (N // P), BANK], F32, "result")
+        absolute = placed_at(14 * row, [P, 2 * (N // P), BANK], F32, "absolute")
         banks = [(ps_c, "acc_c")] * 2 + [(ps_b, "acc_b")] * 2 + [(ps_a, "acc_a")] * 4
         units = [(h, c) for h in (1, 0) for c in range(N // P)]
         accs = [pool.tile([P, BANK], F32, name=tag, tag=tag) for pool, tag in banks]

from contextlib import ExitStack

import concourse.mybir as mybir
from concourse.masks import make_identity

K, K2, T, TB, S, PL, H, N = 1024, 512, 4096, 2048, 1024, 512, 1024, 512
FLOPS = 2 * (K * H * S + K2 * H * PL + H * N * S)

F32 = mybir.dt.float32
BF16 = mybir.dt.bfloat16
I32 = mybir.dt.int32
U32 = mybir.dt.uint32
U16 = mybir.dt.uint16
U8 = mybir.dt.uint8
E4M3 = mybir.dt.float8_e4m3fn_x4
E2M1 = mybir.dt.float4_e2m1fn_x4
ALU = mybir.AluOpType
ACT = mybir.ActivationFunctionType

P = 128
PACK = 4
PASS = P * PACK
BANK = 512
SLICES = H // P
PAGES = 4


def tile_list_saffron_adulteration_scores_kernel(
    tc, tab_words, tab_scales, tab2_words, tab2_scales, offs, offs2, pos1,
    w1_words, w1_scales, gain, w2, micro, wgs, w3, lift, out,
):
    nc = tc.nc
    with ExitStack() as ctx:
        lists = ctx.enter_context(tc.tile_pool(name="lists", bufs=1))
        keep = ctx.enter_context(tc.tile_pool(name="keep", bufs=1))
        two = ctx.enter_context(tc.tile_pool(name="two", bufs=2))
        shared = ctx.enter_context(tc.tile_pool(name="shared", bufs=1))
        four = ctx.enter_context(tc.tile_pool(name="four", bufs=4))
        ps_a = ctx.enter_context(tc.psum_pool(name="ps_a", bufs=4))
        ps_b = ctx.enter_context(tc.psum_pool(name="ps_b", bufs=2))
        ps_c = ctx.enter_context(tc.psum_pool(name="ps_c", bufs=2))

        offs_sb = lists.tile([P, S // 16], U16, name="offs_sb")
        offs2_sb = lists.tile([P, PL // 16], U16, name="offs2_sb")
        pos_sb = lists.tile([P, PL // 16], U16, name="pos_sb")

        def held(shape, dtype, name):
            return keep.tile(shape, dtype, name=name, align_bytes=64)

        tab2_s = held([P, TB], U8, "tab2_s")
        tab_s = held([P, T], U8, "tab_s")
        w1_s_raw = held([P, H], U8, "w1_s_raw")
        tab2_w = held([P, TB], I32, "tab2_w")
        w1_w_raw = held([P, 2, 2 * H], U8, "w1_w_raw")
        warm = held([P, 1], F32, "warm")
        warm_out = held([P, 1], F32, "warm_out")
        pages = [held([P, S], F32, f"page{i}") for i in range(PAGES)]

        def placed_at(offset, shape, dtype, name):
            return shared.tile(shape, dtype, name=name, offset=offset, align_bytes=64)

        row = 4 * BANK
        tab_w = [placed_at(a * 8 * row, [P, T], I32, f"tab_w{a}") for a in range(2)]
        micro_sb = [keep.tile([P, PL], F32, name=f"micro{i}", tag="micro_early")[:] for i in range(2)]
        micro_sb = micro_sb + [placed_at(i * row, [P, PL], F32, f"micro{i}")[:] for i in range(2, PACK)]
        wgs_sb = [held([P, PL], F32, f"wgs{t}") for t in range(PACK)]
        gain_sb = placed_at(5 * row, [P, 2, PACK], F32, "gain_sb")
        lift_sb = placed_at(5 * row + 64, [P, N // P], F32, "lift_sb")
        w2_first = held([P, PACK, PASS], F32, "w2_first")
        w2_raw = [w2_first[:], placed_at(6 * row, [P, PACK, PASS], F32, "w2_second")[:]]
        micro_sb = micro_sb + [placed_at((6 + i) * row, [P, PL], F32, f"micro{i}")[:] for i in range(PACK, SLICES)]
        w3_both = placed_at(14 * row, [P, 2, PACK, N], F32, "w3_both")
        w3_raw = [w3_both[:, b] for b in range(2)]

        def zero_upper(engine, tile):
            words = tile[:].bitcast(I32)
            engine.memset(words[32:64, :], 0)
            engine.memset(words[64:128, :], 0)

        micro_rows = micro.rearrange("(b p t) j -> b t p j", b=2, t=PACK)

        def load_w2(b):
            nc.sync.dma_start(w2_raw[b], w2[:, b * PASS:(b + 1) * PASS].rearrange("(p j) c -> p j c", j=PACK))

        def load_micro(i):
            nc.sync.dma_start(micro_sb[i], micro_rows[i // PACK, i % PACK])

        def load_tab(a):
            nc.sync.dma_start(tab_w[a][:], tab_words[a].rearrange("p t i -> p (t i)").bitcast(I32))

        nc.gpsimd.memset(warm[:], 1.0)
        nc.gpsimd.memset(tab2_s[:].bitcast(I32), 0)
        zero_upper(nc.vector, tab_s)
        identity = held([P, P], F32, "identity")
        make_identity(nc, identity[:])
        zero_upper(nc.gpsimd, w1_s_raw)
        nc.scalar.activation(warm_out[:], warm[:], ACT.Abs_reciprocal_sqrt)
        for q in range(4):
            nc.scalar.dma_start(tab2_s[:].bitcast(I32)[32 * q:32 * q + 4, :], tab2_scales[0, 4 * q:4 * q + 4, :].bitcast(I32))
        nc.sync.dma_start(offs2_sb[:], offs2)
        nc.sync.dma_start(offs_sb[:], offs)
        nc.sync.dma_start(tab_s[:].bitcast(I32)[0:32, :], tab_scales.bitcast(I32).rearrange("a q n -> q a n"))
        nc.sync.dma_start(w1_s_raw[:].bitcast(I32)[0:32, :], w1_scales.bitcast(I32).rearrange("a q n -> q a n"))
        nc.sync.dma_start(pos_sb[:], pos1)
        wgs_raw = held([P, PL], F32, "wgs_raw")
        nc.sync.dma_start(wgs_raw[:], wgs)
        load_w2(0)
        nc.sync.dma_start(tab2_w[:], tab2_words[0].rearrange("p t i -> p (t i)").bitcast(I32))
        load_micro(0)
        load_tab(0)
        nc.sync.dma_start(w1_w_raw[:].bitcast(I32), w1_words.bitcast(I32).rearrange("a p n -> p a n"))
        load_tab(1)
        load_micro(1)
        nc.sync.dma_start(gain_sb[:], gain.rearrange("(b p t) -> p b t", b=2, t=PACK))
        load_micro(2)
        load_micro(3)
        load_w2(1)
        for i in range(PACK, SLICES):
            load_micro(i)
        for b in range(2):
            nc.sync.dma_start(w3_raw[b], w3[b * PASS:(b + 1) * PASS, :].rearrange("(p j) n -> p j n", j=PACK))
        with nc.allow_non_contiguous_dma("one value of lift for each partition"):
            nc.sync.dma_start(lift_sb[:], lift.rearrange("(c p) -> p c", p=P))

        v2_s = held([P, PL], U8, "v2_s")
        planes = held([P, 2, S + H], U8, "planes")
        nc.gpsimd.memset(pages[0][:], 0.0)
        nc.gpsimd.memset(planes[:].bitcast(I32), 0)

        rows = held([P, S + H], U8, "rows")
        v_s_rows = held([P, S], U8, "v_s_rows")
        nc.vector.tensor_copy(v_s_rows[:], tab_s[:].indirect(offs_sb[:]))
        v2_w = held([P, PL], U32, "v2_w")
        nc.vector.tensor_copy(v2_s[:], tab2_s[:].indirect(offs2_sb[:]))
        nc.vector.tensor_copy(v2_w[:], tab2_w[:].bitcast(U32).indirect(offs2_sb[:]))
        nc.vector.tensor_copy(
            rows[:, S:].rearrange("p (b t q) -> p b t q", b=2, t=PACK),
            w1_s_raw[:].rearrange("p (b q t) -> p b t q", b=2, t=PACK),
        )
        nc.vector.tensor_copy(rows[:].bitcast(I32)[:, 0:S // 4], v_s_rows[:].bitcast(I32))
        for q in range(4):
            nc.scalar.dma_start(
                planes[:].rearrange("p a c -> p (a c)").bitcast(I32)[32 * q:32 * q + 4, :],
                rows[:].bitcast(I32)[8 * q:8 * (q + 1), :],
            )
        for i in range(1, PAGES):
            nc.gpsimd.memset(pages[i][:], 0.0)
        w1_w = held([P, 2, 2 * H], U8, "w1_w")
        nc.vector.tensor_copy(
            w1_w[:].rearrange("p a c -> p (a c)").bitcast(U16).rearrange("p (g t q) -> p g t q", g=4, t=PACK),
            w1_w_raw[:].rearrange("p a c -> p (a c)").bitcast(U16).rearrange("p (g q t) -> p g t q", g=4, t=PACK),
        )

        w2_w = [held([P, PASS], U32, f"w2_w{b}") for b in range(2)]
        w2_s = [held([P, PASS], U8, f"w2_s{b}") for b in range(2)]

        def quantise_w2(b):
            rounded = two.tile([P, PACK * PASS], BF16, name="rounded", tag="rounded", align_bytes=64)
            dst = rounded[:].rearrange("p (t m j) -> p m t j", t=PACK, j=PACK)
            src = w2_raw[b].rearrange("p j (m t) -> p m t j", t=PACK)
            nc.scalar.copy(dst, src)
            nc.vector.quantize_mx(out=w2_w[b][:].bitcast(E4M3), scales=w2_s[b][:], in_=rounded[:])

        w3_w = [held([P, N], U32, f"w3_w{b}") for b in range(2)]
        w3_s = [held([P, N], U8, f"w3_s{b}") for b in range(2)]

        def quantise_w3(b):
            rounded = two.tile([P, PACK * N], BF16, name="rounded", tag="rounded", align_bytes=64)
            nc.scalar.copy(
                rounded[:].rearrange("p (c i j) -> p c j i", i=4, j=PACK),
                w3_raw[b].rearrange("p j (c i) -> p c j i", i=4),
            )
            nc.vector.quantize_mx(out=w3_w[b][:].bitcast(E4M3), scales=w3_s[b][:], in_=rounded[:])

        def findings(i):
            b, t = divmod(i, PACK)
            acc = ps_b.tile([P, BANK], F32, name="acc_b", tag="acc_b")
            nc.tensor.matmul_mx(
                out=acc[:], lhsT=w2_w[b][:, t * P:(t + 1) * P].bitcast(E4M3), lhsT_scale=w2_s[b][:, t * P:(t + 1) * P],
                rhs=v2_w[:].bitcast(E4M3), rhs_scale=v2_s[:], start=True, stop=True,
            )
            summed = two.tile([P, PL], F32, name="summed", tag="summed")
            nc.vector.tensor_tensor(summed[:], acc[:], micro_sb[i], ALU.add)
            return summed

        def place(i, summed):
            nc.vector.tensor_tensor(pages[i % PAGES][:].indirect(pos_sb[:]), summed[:], wgs_sb[i % PACK][:], ALU.mult)

        v_w = [held([P, S], U32, f"v_w{a}") for a in range(2)]

        def gather_words(a, lo, hi):
            nc.vector.tensor_copy(v_w[a][:, lo:hi], tab_w[a][:].bitcast(U32).indirect(offs_sb[:, lo // 16:hi // 16]))

        mags = [held([P, S], F32, f"mag{i}") for i in range(2)]
        roots = [held([P, S], F32, f"root{i}") for i in range(2)]

        def response(i):
            mag, root = mags[i % 2], roots[i % 2]
            for h in range(2):
                acc = ps_a.tile([P, BANK], F32, name="acc_a", tag="acc_a")
                for a in range(2):
                    nc.tensor.matmul_mx(
                        out=acc[:],
                        lhsT=w1_w[:, a, 2 * i * P:2 * (i + 1) * P].bitcast(E2M1),
                        lhsT_scale=planes[:, a, S + i * P:S + (i + 1) * P],
                        rhs=v_w[a][:, h * BANK:(h + 1) * BANK].bitcast(E4M3),
                        rhs_scale=planes[:, a, h * BANK:(h + 1) * BANK],
                        start=(a == 0), stop=(a == 1),
                    )
                nc.scalar.activation(mag[:, h * BANK:(h + 1) * BANK], acc[:], ACT.Abs)
            nc.scalar.activation(root[:], mag[:], ACT.Abs_reciprocal_sqrt, bias=1.0)
            recip = four.tile([P, S], F32, name="recip", tag="recip")
            nc.scalar.activation(recip[:], root[:], ACT.Square)
            return recip

        z_rows = [held([P, PACK, S], BF16, f"z_rows{b}") for b in range(2)]

        def subtract(i, recip):
            b, t = divmod(i, PACK)
            pieces = 2 if i == SLICES - 1 else 1
            for u in range(pieces):
                cols = slice(u * S // pieces, (u + 1) * S // pieces)
                nc.vector.scalar_tensor_tensor(
                    z_rows[b][:, t, cols], recip[:, cols], gain_sb[:, b, t:t + 1], pages[i % PAGES][:, cols],
                    ALU.mult, ALU.subtract,
                )

        z_w = [held([P, S], U32, f"z_w{b}") for b in range(2)]
        z_s = [held([P, S], U8, f"z_s{b}") for b in range(2)]

        def weave(b, h, on_scalar):
            woven = (roots, mags)[h][b][:].bitcast(BF16)
            dst = woven.rearrange("p (c i t) -> p c t i", i=4, t=PACK)
            src = z_rows[b][:, :, h * BANK:(h + 1) * BANK].rearrange("p t (c i) -> p c t i", i=4)
            if on_scalar:
                nc.scalar.copy(dst, src)
            else:
                nc.vector.tensor_copy(dst, src)

        def quantise_z(b, h):
            woven = (roots, mags)[h][b][:].bitcast(BF16)
            cols = slice(h * BANK, (h + 1) * BANK)
            nc.vector.quantize_mx(out=z_w[b][:, cols].bitcast(E4M3), scales=z_s[b][:, cols], in_=woven)

        chunks = PL // P
        turned = ps_c.tile([P, chunks, P], F32, name="acc_c", tag="acc_c")
        for c in range(chunks):
            nc.tensor.transpose(turned[:, c, :], wgs_raw[:, c * P:(c + 1) * P], identity[:])
        dealt = held([P, PACK, chunks, P], F32, "dealt")

        def deal_wgs(t):
            nc.scalar.copy(
                dealt[:, t].rearrange("p c (r q) -> p c r q", r=4),
                turned[:].rearrange("p c (q t) -> p t c q", t=PACK)[:, t].unsqueeze(2).to_broadcast([P, chunks, 4, 32]),
            )

        def turn_back_wgs(t):
            back = ps_a.tile([P, chunks, P], F32, name="acc_a", tag="acc_a")
            for c in range(chunks):
                nc.tensor.transpose(back[:, c, :], dealt[:, t, c, :], identity[:])
            nc.scalar.copy(wgs_sb[t][:], back[:].rearrange("p c j -> p (c j)"))

        deal_wgs(0)
        quantise_w2(0)
        turn_back_wgs(0)
        for t in range(1, PACK):
            deal_wgs(t)
            turn_back_wgs(t)
        sums = {0: findings(0)}
        place(0, sums[0])
        gather_words(0, 0, S)
        gather_words(1, 0, BANK)
        gather_words(1, BANK, S)
        for i in range(1, PAGES):
            sums[i] = findings(i)
            place(i, sums[i])
        quantise_w2(1)
        for i in range(SLICES):
            if i == SLICES - 1:
                for h in (1, 0):
                    weave(0, h, True)
                    quantise_z(0, h)
            recip = response(i)
            if i + PAGES < SLICES:
                sums[i + PAGES] = findings(i + PAGES)
            subtract(i, recip)
            if i + PAGES < SLICES:
                place(i + PAGES, sums[i + PAGES])
            if i in (2, 4):
                quantise_w3(i // 2 - 1)
        weave(1, 0, True)
        weave(1, 1, False)
        quantise_z(1, 1)
        quantise_z(1, 0)

        result = placed_at(6 * row, [P, 2 * (N // P), BANK], F32, "result")
        absolute = placed_at(14 * row, [P, 2 * (N // P), BANK], F32, "absolute")
        banks = [(ps_c, "acc_c")] * 2 + [(ps_b, "acc_b")] * 2 + [(ps_a, "acc_a")] * 4
        units = [(h, c) for h in (1, 0) for c in range(N // P)]
        accs = [pool.tile([P, BANK], F32, name=tag, tag=tag) for pool, tag in banks]
        for b in range(2):
            for u, (h, c) in enumerate(units):
                cols = slice(h * BANK, (h + 1) * BANK)
                nc.tensor.matmul_mx(
                    out=accs[u][:], lhsT=w3_w[b][:, c * P:(c + 1) * P].bitcast(E4M3), lhsT_scale=w3_s[b][:, c * P:(c + 1) * P],
                    rhs=z_w[b][:, cols].bitcast(E4M3), rhs_scale=z_s[b][:, cols], start=(b == 0), stop=(b == 1),
                )
        for u, (h, c) in enumerate(units):
            nc.scalar.activation(absolute[:, u, :], accs[u][:], ACT.Abs)
            nc.vector.scalar_tensor_tensor(
                result[:, u, :], absolute[:, u, :], lift_sb[:, c:c + 1], accs[u][:], ALU.mult, ALU.add,
            )
            nc.sync.dma_start(out[c * P:(c + 1) * P, h * BANK:(h + 1) * BANK], result[:, u, :])
